import numpy as np
import ml_dtypes


def mxq(x, axis, fmt="e4m3"):
    dtype, down = {"e4m3": (ml_dtypes.float8_e4m3fn, 7), "e5m2": (ml_dtypes.float8_e5m2, 14)}[fmt]
    v = np.moveaxis(np.asarray(x, np.float32).astype(ml_dtypes.bfloat16).astype(np.float64), axis, -1)
    blocks = v.reshape(v.shape[:-1] + (-1, 32))
    amax = np.abs(blocks).max(-1, keepdims=True)
    byte = np.maximum(np.where(amax > 0, np.frexp(amax)[1] - 1 + 127, 0) - down, 1)
    scale = np.exp2(byte - 127.0)
    codes = (blocks / scale).astype(np.float32).astype(dtype).astype(np.float64)
    return np.moveaxis((codes * scale).reshape(v.shape), -1, axis)


WIDE = False


def mx_kscale(k):
    if not WIDE:
        return np.ones(k)
    levels = np.array([10, -10, 5, -5, 0])
    if k % 512:
        return np.exp2(np.random.permutation(np.resize(levels, k // 32))).repeat(32)
    a = np.empty((k // 512, 16))
    for p in range(k // 512):
        a[p, :8] = np.random.permutation(np.resize(levels, 8))
        for g in range(8):
            far = levels[np.abs(levels - a[p, g]) >= 10]
            a[p, g + 8] = far[np.random.randint(len(far))]
    return np.exp2(a.ravel()).repeat(32)


def f64(x):
    return np.asarray(x).astype(np.float64)


def striped(idx):
    return np.tile(idx.reshape(-1, 16).T, (8, 1)).astype(np.uint16)


def unstriped(offs):
    return offs[:16].T.reshape(-1).astype(np.int64)


K, T, S, N = 512, 4096, 1024, 512


def setup_inputs():
    n = np.random.standard_normal
    s = mx_kscale(K)[:, None]
    w1, w2 = n((2, K, N)) / np.sqrt(2 * K) / s[None]
    return {
        "xT": (n((K, S)) * s).astype(np.float32),
        "sT": (n((K, T)) * s).astype(np.float32),
        "w1": w1.astype(np.float32),
        "w2": w2.astype(np.float32),
        "offs": striped(np.random.permutation(T)[:S]),
    }


def reference(xT, sT, w1, w2, offs):
    y = mxq(f64(w1), 0, "e4m3").T @ mxq(f64(xT), 0, "e4m3") + mxq(f64(w2), 0, "e4m3").T @ mxq(f64(sT)[:, unstriped(offs)], 0, "e4m3")
    return y

@@ -1,0 +1,141 @@
+from contextlib import ExitStack
+
+import concourse.mybir as mybir
+
+K, T, S, N = 512, 4096, 1024, 512
+FLOPS = 2 * 2 * K * S * N
+
+F32 = mybir.dt.float32
+BF16 = mybir.dt.bfloat16
+U32 = mybir.dt.uint32
+U16 = mybir.dt.uint16
+U8 = mybir.dt.uint8
+FP8X4 = mybir.dt.float8_e4m3fn_x4
+COPY = mybir.ActivationFunctionType.Copy
+
+P = 128
+PACK = 4
+HALF = S // 2
+M_BLOCKS = N // P
+
+
+def tile_picked_recall_none_e_kernel(tc, xT, sT, w1, w2, offs, out):
+    nc = tc.nc
+    with ExitStack() as ctx:
+        lists = ctx.enter_context(tc.tile_pool(name="lists", bufs=1))
+        keep = ctx.enter_context(tc.tile_pool(name="keep", bufs=1))
+        psum = ctx.enter_context(tc.psum_pool(name="psum", bufs=1))
+
+        offsets = lists.tile([P, S // 16], U16, name="offsets")
+
+        x_rows = xT.rearrange("(p j) c -> p j c", j=PACK)
+        s_rows = sT.rearrange("(p j) t -> p j t", j=PACK)
+        w_raw = {}
+        for i, w in ((2, w2), (1, w1)):
+            w_raw[i] = keep.tile([P, PACK, N], F32, name="w_raw%d" % i)
+            nc.sync.dma_start(out=w_raw[i][:], in_=w.rearrange("(p j) c -> p j c", j=PACK))
+            if i == 2:
+                nc.sync.dma_start(offsets[:], offs)
+        planes = [keep.tile([P, T], F32, name="plane%d" % j) for j in range(PACK)]
+        x_raw = [keep.tile([P, PACK, HALF], F32, name="x_raw%d" % h) for h in range(2)]
+
+        def load_plane(j):
+            nc.sync.dma_start(out=planes[j][:], in_=s_rows[:, j, :])
+
+        def load_x(h, c0, c1):
+            nc.sync.dma_start(out=x_raw[h][:, :, c0:c1], in_=x_rows[:, :, h * HALF + c0 : h * HALF + c1])
+
+        def load_plane_part(j, t0, t1):
+            nc.sync.dma_start(out=planes[j][:, t0:t1], in_=s_rows[:, j, t0:t1])
+
+        load_plane(0)
+        load_plane(1)
+        load_plane(2)
+        load_plane_part(3, 0, T // 2)
+        load_x(0, 0, HALF)
+        load_plane_part(3, T // 2, T)
+        load_x(1, 0, 256)
+        load_x(1, 256, 512)
+
+        def interleave(engine, grouped, raw, c0, c1):
+            dst = grouped[:, c0:c1, :]
+            src = raw[:, :, c0:c1].rearrange("p j c -> p c j")
+            if engine == "v":
+                nc.vector.tensor_copy(out=dst, in_=src)
+            elif engine == "g":
+                nc.gpsimd.tensor_copy(out=dst, in_=src)
+            else:
+                nc.scalar.copy(out=dst, in_=src)
+
+        def operand(name):
+            codes = keep.tile([P, HALF], U32, name=name + "_codes", align_bytes=64)
+            scales = keep.tile([P, HALF], U8, name=name + "_scales", align_bytes=64)
+            return codes, scales
+
+        def quantize(op, grouped, c0=0, c1=HALF):
+            nc.vector.quantize_mx(
+                out=op[0][:, c0:c1].bitcast(FP8X4),
+                scales=op[1][:, c0:c1],
+                in_=grouped[:, c0:c1, :].rearrange("p c j -> p (c j)"),
+            )
+
+        def mx(acc, w, rhs, m, start, stop, c0=0, c1=HALF):
+            cols = slice(m * P, (m + 1) * P)
+            nc.tensor.matmul_mx(
+                out=acc[:, c0:c1],
+                lhsT=w[0][:, cols].bitcast(FP8X4),
+                lhsT_scale=w[1][:, cols],
+                rhs=rhs[0][:, c0:c1].bitcast(FP8X4),
+                rhs_scale=rhs[1][:, c0:c1],
+                start=start,
+                stop=stop,
+            )
+
+        def leave(engine, acc, h, m, c0=0, c1=HALF):
+            result = keep.tile([P, c1 - c0], F32, name="result%d_%d_%d" % (h, m, c0))
+            if engine == "v":
+                nc.vector.tensor_copy(out=result[:], in_=acc[:, c0:c1])
+            else:
+                nc.scalar.copy(out=result[:], in_=acc[:, c0:c1])
+            nc.sync.dma_start(out=out[m * P : (m + 1) * P, h * HALF + c0 : h * HALF + c1], in_=result[:])
+
+        w_op = {}
+        for i in (2, 1):
+            grouped = keep.tile([P, N, PACK], BF16, name="w_grouped%d" % i, align_bytes=64)
+            interleave("s", grouped, w_raw[i], 0, N)
+            w_op[i] = operand("w%d" % i)
+            quantize(w_op[i], grouped)
+
+        s_grouped = [keep.tile([P, HALF, PACK], BF16, name="s_grouped%d" % h, align_bytes=64) for h in range(2)]
+        s_op = [operand("s%d" % h) for h in range(2)]
+        x_grouped = [keep.tile([P, HALF, PACK], BF16, name="x_grouped%d" % h, align_bytes=64) for h in range(2)]
+        x_op = [operand("x%d" % h) for h in range(2)]
+        accs = [[psum.tile([P, HALF], F32, name="acc%d_%d" % (h, m)) for m in range(M_BLOCKS)] for h in range(2)]
+
+        def gather(j, h):
+            half_list = offsets[:, h * (HALF // 16) : (h + 1) * (HALF // 16)]
+            nc.vector.tensor_copy(out=s_grouped[h][:, :, j], in_=planes[j][:].indirect(half_list))
+
+        for j in (0, 1, 2):
+            gather(j, 0)
+            gather(j, 1)
+        interleave("s", x_grouped[0], x_raw[0], 0, 256)
+        interleave("v", x_grouped[0], x_raw[0], 256, 512)
+        quantize(x_op[0], x_grouped[0])
+        for m in range(M_BLOCKS):
+            mx(accs[0][m], w_op[1], x_op[0], m, True, False)
+        gather(3, 0)
+        quantize(s_op[0], s_grouped[0])
+        interleave("s", x_grouped[1], x_raw[1], 0, 256)
+        interleave("g", x_grouped[1], x_raw[1], 256, 512)
+        for m in range(M_BLOCKS):
+            mx(accs[0][m], w_op[2], s_op[0], m, False, True)
+            leave("s", accs[0][m], 0, m)
+        gather(3, 1)
+        quantize(s_op[1], s_grouped[1])
+        quantize(x_op[1], x_grouped[1])
+        for m in range(M_BLOCKS):
+            mx(accs[1][m], w_op[2], s_op[1], m, True, False)
+        for m in range(M_BLOCKS):
+            mx(accs[1][m], w_op[1], x_op[1], m, False, True)
+            leave("v" if m % 2 else "s", accs[1][m], 1, m)

@@ -11,12 +11,12 @@ U32 = mybir.dt.uint32
 U16 = mybir.dt.uint16
 U8 = mybir.dt.uint8
 FP8X4 = mybir.dt.float8_e4m3fn_x4
-COPY = mybir.ActivationFunctionType.Copy
 
 P = 128
 PACK = 4
 HALF = S // 2
 M_BLOCKS = N // P
+UNIT = 256
 
 
 def tile_picked_recall_none_e_kernel(tc, xT, sT, w1, w2, offs, out):
@@ -36,106 +36,97 @@ def tile_picked_recall_none_e_kernel(tc, xT, sT, w1, w2, offs, out):
             nc.sync.dma_start(out=w_raw[i][:], in_=w.rearrange("(p j) c -> p j c", j=PACK))
             if i == 2:
                 nc.sync.dma_start(offsets[:], offs)
-        planes = [keep.tile([P, T], F32, name="plane%d" % j) for j in range(PACK)]
-        x_raw = [keep.tile([P, PACK, HALF], F32, name="x_raw%d" % h) for h in range(2)]
+        planes = []
+        for j in range(PACK):
+            plane = keep.tile([P, T], F32, name="plane%d" % j)
+            nc.sync.dma_start(out=plane[:], in_=s_rows[:, j, :])
+            planes.append(plane)
+        x_raw = keep.tile([P, PACK, S], F32, name="x_raw")
+        for c0, c1 in ((0, 256), (256, 512), (512, 1024)):
+            nc.sync.dma_start(out=x_raw[:, :, c0:c1], in_=x_rows[:, :, c0:c1])
 
-        def load_plane(j):
-            nc.sync.dma_start(out=planes[j][:], in_=s_rows[:, j, :])
+        def operand(name, width):
+            grouped = keep.tile([P, width, PACK], BF16, name=name + "_grouped", align_bytes=64)
+            codes = keep.tile([P, width], U32, name=name + "_codes", align_bytes=64)
+            scales = keep.tile([P, width], U8, name=name + "_scales", align_bytes=64)
+            return grouped, codes, scales
 
-        def load_x(h, c0, c1):
-            nc.sync.dma_start(out=x_raw[h][:, :, c0:c1], in_=x_rows[:, :, h * HALF + c0 : h * HALF + c1])
+        def interleave(copy, op, raw, c0, c1):
+            copy(out=op[0][:, c0:c1, :], in_=raw[:, :, c0:c1].rearrange("p j c -> p c j"))
 
-        def load_plane_part(j, t0, t1):
-            nc.sync.dma_start(out=planes[j][:, t0:t1], in_=s_rows[:, j, t0:t1])
-
-        load_plane(0)
-        load_plane(1)
-        load_plane(2)
-        load_plane_part(3, 0, T // 2)
-        load_x(0, 0, HALF)
-        load_plane_part(3, T // 2, T)
-        load_x(1, 0, 256)
-        load_x(1, 256, 512)
-
-        def interleave(engine, grouped, raw, c0, c1):
-            dst = grouped[:, c0:c1, :]
-            src = raw[:, :, c0:c1].rearrange("p j c -> p c j")
-            if engine == "v":
-                nc.vector.tensor_copy(out=dst, in_=src)
-            elif engine == "g":
-                nc.gpsimd.tensor_copy(out=dst, in_=src)
-            else:
-                nc.scalar.copy(out=dst, in_=src)
-
-        def operand(name):
-            codes = keep.tile([P, HALF], U32, name=name + "_codes", align_bytes=64)
-            scales = keep.tile([P, HALF], U8, name=name + "_scales", align_bytes=64)
-            return codes, scales
-
-        def quantize(op, grouped, c0=0, c1=HALF):
+        def quantize(op, c0, c1):
             nc.vector.quantize_mx(
-                out=op[0][:, c0:c1].bitcast(FP8X4),
-                scales=op[1][:, c0:c1],
-                in_=grouped[:, c0:c1, :].rearrange("p c j -> p (c j)"),
+                out=op[1][:, c0:c1].bitcast(FP8X4),
+                scales=op[2][:, c0:c1],
+                in_=op[0][:, c0:c1, :].rearrange("p c j -> p (c j)"),
             )
 
-        def mx(acc, w, rhs, m, start, stop, c0=0, c1=HALF):
-            cols = slice(m * P, (m + 1) * P)
+        def gather(h, j):
+            nc.vector.tensor_copy(
+                out=s_op[0][:, h * HALF : (h + 1) * HALF, j],
+                in_=planes[j][:].indirect(offsets[:, h * HALF // 16 : (h + 1) * HALF // 16]),
+            )
+
+        def mx(acc, w, op, m, c0, start):
+            rows = slice(m * P, (m + 1) * P)
+            cols = slice(c0, c0 + UNIT)
             nc.tensor.matmul_mx(
-                out=acc[:, c0:c1],
-                lhsT=w[0][:, cols].bitcast(FP8X4),
-                lhsT_scale=w[1][:, cols],
-                rhs=rhs[0][:, c0:c1].bitcast(FP8X4),
-                rhs_scale=rhs[1][:, c0:c1],
+                out=acc[:],
+                lhsT=w[1][:, rows].bitcast(FP8X4),
+                lhsT_scale=w[2][:, rows],
+                rhs=op[1][:, cols].bitcast(FP8X4),
+                rhs_scale=op[2][:, cols],
                 start=start,
-                stop=stop,
+                stop=not start,
             )
-
-        def leave(engine, acc, h, m, c0=0, c1=HALF):
-            result = keep.tile([P, c1 - c0], F32, name="result%d_%d_%d" % (h, m, c0))
-            if engine == "v":
-                nc.vector.tensor_copy(out=result[:], in_=acc[:, c0:c1])
-            else:
-                nc.scalar.copy(out=result[:], in_=acc[:, c0:c1])
-            nc.sync.dma_start(out=out[m * P : (m + 1) * P, h * HALF + c0 : h * HALF + c1], in_=result[:])
 
         w_op = {}
         for i in (2, 1):
-            grouped = keep.tile([P, N, PACK], BF16, name="w_grouped%d" % i, align_bytes=64)
-            interleave("s", grouped, w_raw[i], 0, N)
-            w_op[i] = operand("w%d" % i)
-            quantize(w_op[i], grouped)
+            w_op[i] = operand("w%d" % i, N)
+            interleave(nc.scalar.copy, w_op[i], w_raw[i], 0, N)
+            quantize(w_op[i], 0, N)
+        s_op = operand("s", S)
+        x_op = operand("x", S)
 
-        s_grouped = [keep.tile([P, HALF, PACK], BF16, name="s_grouped%d" % h, align_bytes=64) for h in range(2)]
-        s_op = [operand("s%d" % h) for h in range(2)]
-        x_grouped = [keep.tile([P, HALF, PACK], BF16, name="x_grouped%d" % h, align_bytes=64) for h in range(2)]
-        x_op = [operand("x%d" % h) for h in range(2)]
-        accs = [[psum.tile([P, HALF], F32, name="acc%d_%d" % (h, m)) for m in range(M_BLOCKS)] for h in range(2)]
+        for j in range(3):
+            gather(0, j)
+            gather(1, j)
 
-        def gather(j, h):
-            half_list = offsets[:, h * (HALF // 16) : (h + 1) * (HALF // 16)]
-            nc.vector.tensor_copy(out=s_grouped[h][:, :, j], in_=planes[j][:].indirect(half_list))
+        def first(u):
+            accs = [psum.tile([P, UNIT], F32, name="acc%d_%d" % (u, m), tag="bank%d_%d" % (u % 2, m)) for m in range(M_BLOCKS)]
+            for m in range(M_BLOCKS):
+                mx(accs[m], w_op[2], s_op, m, u * UNIT, True)
+            return accs
 
-        for j in (0, 1, 2):
-            gather(j, 0)
-            gather(j, 1)
-        interleave("s", x_grouped[0], x_raw[0], 0, 256)
-        interleave("v", x_grouped[0], x_raw[0], 256, 512)
-        quantize(x_op[0], x_grouped[0])
-        for m in range(M_BLOCKS):
-            mx(accs[0][m], w_op[1], x_op[0], m, True, False)
-        gather(3, 0)
-        quantize(s_op[0], s_grouped[0])
-        interleave("s", x_grouped[1], x_raw[1], 0, 256)
-        interleave("g", x_grouped[1], x_raw[1], 256, 512)
-        for m in range(M_BLOCKS):
-            mx(accs[0][m], w_op[2], s_op[0], m, False, True)
-            leave("s", accs[0][m], 0, m)
-        gather(3, 1)
-        quantize(s_op[1], s_grouped[1])
-        quantize(x_op[1], x_grouped[1])
-        for m in range(M_BLOCKS):
-            mx(accs[1][m], w_op[2], s_op[1], m, True, False)
-        for m in range(M_BLOCKS):
-            mx(accs[1][m], w_op[1], x_op[1], m, False, True)
-            leave("v" if m % 2 else "s", accs[1][m], 1, m)
+        def second(u, accs, copies):
+            for m in range(M_BLOCKS):
+                mx(accs[m], w_op[1], x_op, m, u * UNIT, False)
+                result = keep.tile([P, UNIT], F32, name="result%d_%d" % (u, m))
+                copies[m](out=result[:], in_=accs[m][:])
+                nc.sync.dma_start(out=out[m * P : (m + 1) * P, u * UNIT : (u + 1) * UNIT], in_=result[:])
+
+        v, s = nc.vector.tensor_copy, nc.scalar.copy
+
+        interleave(s, x_op, x_raw, 0, 128)
+        interleave(v, x_op, x_raw, 128, 256)
+        gather(0, 3)
+        quantize(s_op, 0, 256)
+        quantize(x_op, 0, 256)
+        accs = first(0)
+        second(0, accs, [s, s, s, s])
+        interleave(s, x_op, x_raw, 256, 512)
+        gather(1, 3)
+        quantize(s_op, 256, 512)
+        quantize(x_op, 256, 512)
+        accs = first(1)
+        interleave(v, x_op, x_raw, 512, 768)
+        second(1, accs, [s, s, s, s])
+        quantize(s_op, 512, 768)
+        quantize(x_op, 512, 768)
+        accs = first(2)
+        second(2, accs, [s, s, s, v])
+        interleave(v, x_op, x_raw, 768, 1024)
+        quantize(s_op, 768, 1024)
+        quantize(x_op, 768, 1024)
+        accs = first(3)
+        second(3, accs, [v, s, v, s])

from contextlib import ExitStack

import concourse.mybir as mybir

K, T, S, N = 512, 4096, 1024, 512
FLOPS = 2 * 2 * K * S * N

F32 = mybir.dt.float32
BF16 = mybir.dt.bfloat16
U32 = mybir.dt.uint32
U16 = mybir.dt.uint16
U8 = mybir.dt.uint8
FP8X4 = mybir.dt.float8_e4m3fn_x4

P = 128
PACK = 4
HALF = S // 2
M_BLOCKS = N // P
UNIT = 256


def tile_picked_recall_none_e_kernel(tc, xT, sT, w1, w2, offs, out):
    nc = tc.nc
    with ExitStack() as ctx:
        lists = ctx.enter_context(tc.tile_pool(name="lists", bufs=1))
        keep = ctx.enter_context(tc.tile_pool(name="keep", bufs=1))
        psum = ctx.enter_context(tc.psum_pool(name="psum", bufs=1))

        offsets = lists.tile([P, S // 16], U16, name="offsets")

        x_rows = xT.rearrange("(p j) c -> p j c", j=PACK)
        s_rows = sT.rearrange("(p j) t -> p j t", j=PACK)
        w_raw = {}
        for i, w in ((2, w2), (1, w1)):
            w_raw[i] = keep.tile([P, PACK, N], F32, name="w_raw%d" % i)
            nc.sync.dma_start(out=w_raw[i][:], in_=w.rearrange("(p j) c -> p j c", j=PACK))
            if i == 2:
                nc.sync.dma_start(offsets[:], offs)
        planes = []
        for j in range(PACK):
            plane = keep.tile([P, T], F32, name="plane%d" % j)
            nc.sync.dma_start(out=plane[:], in_=s_rows[:, j, :])
            planes.append(plane)
        x_raw = keep.tile([P, PACK, S], F32, name="x_raw")
        for c0, c1 in ((0, 256), (256, 512), (512, 1024)):
            nc.sync.dma_start(out=x_raw[:, :, c0:c1], in_=x_rows[:, :, c0:c1])

        def operand(name, width):
            grouped = keep.tile([P, width, PACK], BF16, name=name + "_grouped", align_bytes=64)
            codes = keep.tile([P, width], U32, name=name + "_codes", align_bytes=64)
            scales = keep.tile([P, width], U8, name=name + "_scales", align_bytes=64)
            return grouped, codes, scales

        def interleave(copy, op, raw, c0, c1):
            copy(out=op[0][:, c0:c1, :], in_=raw[:, :, c0:c1].rearrange("p j c -> p c j"))

        def quantize(op, c0, c1):
            nc.vector.quantize_mx(
                out=op[1][:, c0:c1].bitcast(FP8X4),
                scales=op[2][:, c0:c1],
                in_=op[0][:, c0:c1, :].rearrange("p c j -> p (c j)"),
            )

        def gather(h, j):
            nc.vector.tensor_copy(
                out=s_op[0][:, h * HALF : (h + 1) * HALF, j],
                in_=planes[j][:].indirect(offsets[:, h * HALF // 16 : (h + 1) * HALF // 16]),
            )

        def mx(acc, w, op, m, c0, start):
            rows = slice(m * P, (m + 1) * P)
            cols = slice(c0, c0 + UNIT)
            nc.tensor.matmul_mx(
                out=acc[:],
                lhsT=w[1][:, rows].bitcast(FP8X4),
                lhsT_scale=w[2][:, rows],
                rhs=op[1][:, cols].bitcast(FP8X4),
                rhs_scale=op[2][:, cols],
                start=start,
                stop=not start,
            )

        w_op = {}
        for i in (2, 1):
            w_op[i] = operand("w%d" % i, N)
            interleave(nc.scalar.copy, w_op[i], w_raw[i], 0, N)
            quantize(w_op[i], 0, N)
        s_op = operand("s", S)
        x_op = operand("x", S)

        for j in range(3):
            gather(0, j)
            gather(1, j)

        def first(u):
            accs = [psum.tile([P, UNIT], F32, name="acc%d_%d" % (u, m), tag="bank%d_%d" % (u % 2, m)) for m in range(M_BLOCKS)]
            for m in range(M_BLOCKS):
                mx(accs[m], w_op[2], s_op, m, u * UNIT, True)
            return accs

        def second(u, accs, copies):
            for m in range(M_BLOCKS):
                mx(accs[m], w_op[1], x_op, m, u * UNIT, False)
                result = keep.tile([P, UNIT], F32, name="result%d_%d" % (u, m))
                copies[m](out=result[:], in_=accs[m][:])
                nc.sync.dma_start(out=out[m * P : (m + 1) * P, u * UNIT : (u + 1) * UNIT], in_=result[:])

        v, s = nc.vector.tensor_copy, nc.scalar.copy

        interleave(s, x_op, x_raw, 0, 128)
        interleave(v, x_op, x_raw, 128, 256)
        gather(0, 3)
        quantize(s_op, 0, 256)
        quantize(x_op, 0, 256)
        accs = first(0)
        second(0, accs, [s, s, s, s])
        interleave(s, x_op, x_raw, 256, 512)
        gather(1, 3)
        quantize(s_op, 256, 512)
        quantize(x_op, 256, 512)
        accs = first(1)
        interleave(v, x_op, x_raw, 512, 768)
        second(1, accs, [s, s, s, s])
        quantize(s_op, 512, 768)
        quantize(x_op, 512, 768)
        accs = first(2)
        second(2, accs, [s, s, s, v])
        interleave(v, x_op, x_raw, 768, 1024)
        quantize(s_op, 768, 1024)
        quantize(x_op, 768, 1024)
        accs = first(3)
        second(3, accs, [v, s, v, s])
